import numpy as np
import ml_dtypes


def mxq(x, axis, fmt="e4m3"):
    dtype, down = {"e4m3": (ml_dtypes.float8_e4m3fn, 7), "e5m2": (ml_dtypes.float8_e5m2, 14)}[fmt]
    v = np.moveaxis(np.asarray(x, np.float32).astype(ml_dtypes.bfloat16).astype(np.float64), axis, -1)
    blocks = v.reshape(v.shape[:-1] + (-1, 32))
    amax = np.abs(blocks).max(-1, keepdims=True)
    byte = np.maximum(np.where(amax > 0, np.frexp(amax)[1] - 1 + 127, 0) - down, 1)
    scale = np.exp2(byte - 127.0)
    codes = (blocks / scale).astype(np.float32).astype(dtype).astype(np.float64)
    return np.moveaxis((codes * scale).reshape(v.shape), -1, axis)


WIDE = False


def mx_kscale(k, group=512):
    if not WIDE:
        return np.ones(k)
    levels = np.array([18, -18])
    if group != 512:
        return np.exp2(np.random.permutation(np.resize(levels, k // group))).repeat(group)
    if k % 512:
        return np.exp2(np.random.permutation(np.resize(levels, k // 32))).repeat(32)
    a = np.empty((k // 512, 16))
    for p in range(k // 512):
        a[p, :8] = np.random.permutation(np.resize(levels, 8))
        for g in range(8):
            far = levels[np.abs(levels - a[p, g]) >= 10]
            a[p, g + 8] = far[np.random.randint(len(far))]
    return np.exp2(a.ravel()).repeat(32)


def f64(x):
    return np.asarray(x).astype(np.float64)


G, D, M, O, N = 4, 128, 128, 128, 512


def setup_inputs():
    n = np.random.standard_normal
    s_d = mx_kscale(D, 0)
    s_o = mx_kscale(O, 0)
    return {
        "x": (n((G, D, N)) * s_d[:, None]).astype(np.float32),
        "w1": (n((G, D, M)) / np.sqrt(D) / s_d[:, None]).astype(np.float32),
        "w2": (n((G, D, M)) / np.sqrt(D) / s_d[:, None]).astype(np.float32),
        "so": (np.random.uniform(0.3, 1.0, (G, M, 1))).astype(np.float32),
        "wo": (n((G, O, M)) / np.sqrt(O) / s_o[:, None]).astype(np.float32),
        "dy": (n((G, O, N)) * s_o[:, None]).astype(np.float32),
        "old": (0.3 * n((G, M, N))).astype(np.float32),
    }


def reference(x, w1, w2, so, wo, dy, old):
    w1q = mxq(f64(w1), 1, "e4m3")
    xq = mxq(f64(x), 1, "e4m3")
    z1 = w1q.transpose(0, 2, 1) @ xq
    w2q = mxq(f64(w2), 1, "e4m3")
    z2 = w2q.transpose(0, 2, 1) @ xq
    nm = np.sqrt(np.square(z1) * np.square(z2) + f64(so))
    woq = mxq(f64(wo), 1, "e4m3")
    dyq = mxq(f64(dy), 1, "e4m3")
    c0 = woq.transpose(0, 2, 1) @ dyq
    dnm = c0 * z1 * z2 / np.square(nm) * (-1.0)
    dz1 = c0 / nm * z2 + dnm * 0.5 / np.sqrt(np.square(z1) * np.square(z2) + f64(so)) * np.square(z2) * z1 * 2.0
    y = dz1 + f64(old)
    return y

@@ -1,0 +1,195 @@
+from contextlib import ExitStack
+
+import concourse.mybir as mybir
+
+G, D, M, N = 4, 128, 128, 512
+FLOPS = 3 * 2 * G * D * M * N
+
+F32 = mybir.dt.float32
+BF16 = mybir.dt.bfloat16
+U32 = mybir.dt.uint32
+U8 = mybir.dt.uint8
+FP8X4 = mybir.dt.float8_e4m3fn_x4
+ALU = mybir.AluOpType
+ACT = mybir.ActivationFunctionType
+
+P = 128
+PACK = 4
+ROWS = D // PACK
+HALF = N // 2
+X_SPLIT = 352
+
+
+def tile_rows_bagree_kernel(tc, x, w1, w2, so, wo, dy, old, out):
+    nc = tc.nc
+    with ExitStack() as ctx:
+        sb = ctx.enter_context(tc.tile_pool(name="sb", bufs=1))
+        ps = ctx.enter_context(tc.psum_pool(name="ps", bufs=1))
+        ctx.enter_context(tc.manual_schedule())
+
+        def load(name, src):
+            width = src.shape[2]
+            raw = sb.tile([P, PACK, width], F32, name=name + "_raw", align_bytes=64)
+            nc.sync.dma_start(out=raw[:], in_=src.rearrange("g (p j) w -> (g p) j w", j=PACK))
+            grouped = sb.tile([P, width, PACK], BF16, name=name + "_bf", align_bytes=64)
+            codes = sb.tile([P, width], U32, name=name + "_codes", align_bytes=64)
+            scales = sb.tile([P, width], U8, name=name + "_scales", align_bytes=64)
+            return raw, grouped, codes, scales
+
+        def interleave(copy, op, lo, hi):
+            raw, grouped = op[0], op[1]
+            copy(
+                out=grouped[:, lo:hi, :].rearrange("p (c i) j -> p c j i", i=4),
+                in_=raw[:, :, lo:hi].rearrange("p j (c i) -> p c j i", i=4),
+            )
+
+        def quantize(op):
+            nc.vector.quantize_mx(
+                out=op[2][:].bitcast(FP8X4), scales=op[3][:], in_=op[1][:].rearrange("p w j -> p (w j)")
+            )
+
+        def product(bank, g, w, a):
+            rows = slice(ROWS * g, ROWS * (g + 1))
+            nc.tensor.matmul_mx(
+                out=bank[:],
+                lhsT=w[2][rows, :].bitcast(FP8X4),
+                lhsT_scale=w[3][rows, :],
+                rhs=a[2][rows, :].bitcast(FP8X4),
+                rhs_scale=a[3][rows, :],
+                start=True,
+                stop=True,
+            )
+
+        so_rows = sb.tile([P, P], F32, align_bytes=64)
+        so_cols = sb.tile([P, P], F32, align_bytes=64)
+        nc.vector.memset(so_rows[:], 0.0)
+        nc.scalar.dma_start(
+            out=so_rows[0:P:32, :].rearrange("q (g i) -> q g i", g=G),
+            in_=so.rearrange("g (q i) o -> q g (i o)", i=32),
+        )
+        warm_in = sb.tile([P, 8], F32)
+        warm_out = sb.tile([P, 8], F32)
+        nc.vector.memset(warm_in[:], 1.0)
+        nc.scalar.activation(out=warm_out[:], in_=warm_in[:], func=ACT.Abs_reciprocal_sqrt)
+
+        xq = load("x", x)
+        w2q = load("w2", w2)
+        w1q = load("w1", w1)
+        woq = load("wo", wo)
+        dyq = load("dy", dy)
+        old_sb = sb.tile([P, G, N], F32)
+        nc.sync.dma_start(out=old_sb[:], in_=old.rearrange("g m n -> m g n"))
+
+        bank_a = [ps.tile([P, N], F32, name="bank_a%d" % g) for g in range(G)]
+        bank_b = [ps.tile([P, N], F32, name="bank_b%d" % g) for g in range(G)]
+
+        def tiles(name):
+            return [sb.tile([P, N], F32, name="%s%d" % (name, g)) for g in range(G)]
+
+        z2 = tiles("z2")
+        prod = tiles("prod")
+        prod_sq = tiles("prod_sq")
+        r = tiles("r")
+        r_sq = tiles("r_sq")
+        r_cu = tiles("r_cu")
+        t = tiles("t")
+        dz1 = tiles("dz1")
+        res = tiles("res")
+        halves = [slice(0, HALF), slice(HALF, N)]
+
+        def soft(g):
+            return so_cols[:, 32 * g : 32 * g + 1]
+
+        interleave(nc.vector.tensor_copy, xq, 0, X_SPLIT)
+        interleave(nc.scalar.copy, xq, X_SPLIT, N)
+        interleave(nc.scalar.copy, w2q, 0, M)
+        quantize(xq)
+        interleave(nc.vector.tensor_copy, w1q, 0, M)
+        quantize(w2q)
+        quantize(w1q)
+        interleave(nc.scalar.copy, woq, 0, M)
+        nc.vector.transpose(out=so_cols[:], in_=so_rows[:])
+        quantize(woq)
+        for g in range(G):
+            product(bank_a[g], g, w2q, xq)
+            product(bank_b[g], g, w1q, xq)
+
+        def copy_z2(g):
+            nc.scalar.copy(out=z2[g][:], in_=bank_a[g][:])
+
+        def make_prod(g):
+            nc.vector.tensor_tensor(out=prod[g][:], in0=bank_b[g][:], in1=z2[g][:], op=ALU.mult)
+
+        def roots(g):
+            for h in halves:
+                nc.scalar.activation(out=prod_sq[g][:, h], in_=prod[g][:, h], func=ACT.Square)
+            for h in halves:
+                nc.scalar.activation(out=r[g][:, h], in_=prod_sq[g][:, h], func=ACT.Abs_reciprocal_sqrt, bias=soft(g))
+            for h in halves:
+                nc.scalar.activation(out=r_sq[g][:, h], in_=r[g][:, h], func=ACT.Square)
+
+        def cube(g, h):
+            nc.gpsimd.tensor_tensor(out=r_cu[g][:, h], in0=r[g][:, h], in1=r_sq[g][:, h], op=ALU.mult)
+
+        def grad(g):
+            for h in halves:
+                nc.vector.scalar_tensor_tensor(
+                    out=t[g][:, h], in0=bank_a[g][:, h], scalar=soft(g), in1=r_cu[g][:, h], op0=ALU.mult, op1=ALU.mult
+                )
+            for h in halves:
+                nc.vector.tensor_tensor(out=dz1[g][:, h], in0=bank_b[g][:, h], in1=t[g][:, h], op=ALU.mult)
+
+        def add_old(eng, g, h):
+            eng.tensor_tensor(out=res[g][:, h], in0=dz1[g][:, h], in1=old_sb[:, g, h], op=ALU.add)
+
+        def store(g, h):
+            nc.sync.dma_start(out=out[g, :, h], in_=res[g][:, h])
+
+        whole = slice(0, N)
+        h0, h1 = halves
+        copy_z2(0)
+        make_prod(0)
+        copy_z2(1)
+        make_prod(1)
+        roots(0)
+        interleave(nc.vector.tensor_copy, dyq, 0, N)
+        copy_z2(2)
+        make_prod(2)
+        quantize(dyq)
+        product(bank_b[0], 0, woq, dyq)
+        product(bank_b[1], 1, woq, dyq)
+        product(bank_b[2], 2, woq, dyq)
+        cube(0, h0)
+        cube(0, h1)
+        roots(1)
+        grad(0)
+        copy_z2(3)
+        make_prod(3)
+        product(bank_b[3], 3, woq, dyq)
+        add_old(nc.gpsimd, 0, h0)
+        cube(1, h0)
+        cube(1, h1)
+        add_old(nc.gpsimd, 0, h1)
+        store(0, whole)
+        roots(2)
+        grad(1)
+        add_old(nc.gpsimd, 1, h0)
+        cube(2, h0)
+        cube(2, h1)
+        add_old(nc.gpsimd, 1, h1)
+        store(1, whole)
+        nc.vector.scalar_tensor_tensor(
+            out=r_cu[3][:], in0=bank_b[3][:], scalar=soft(3), in1=z2[3][:], op0=ALU.mult, op1=ALU.mult
+        )
+        roots(3)
+        grad(2)
+        add_old(nc.gpsimd, 2, h0)
+        add_old(nc.gpsimd, 2, h1)
+        store(2, whole)
+        for h in halves:
+            nc.vector.tensor_tensor(out=t[3][:, h], in0=r_cu[3][:, h], in1=r[3][:, h], op=ALU.mult)
+        for h in halves:
+            nc.vector.tensor_tensor(out=dz1[3][:, h], in0=t[3][:, h], in1=r_sq[3][:, h], op=ALU.mult)
+        for h in halves:
+            add_old(nc.vector, 3, h)
+            store(3, h)

@@ -129,7 +129,7 @@ def tile_rows_bagree_kernel(tc, x, w1, w2, so, wo, dy, old, out):
                 nc.scalar.activation(out=r_sq[g][:, h], in_=r[g][:, h], func=ACT.Square)
 
         def cube(g, h):
-            nc.gpsimd.tensor_tensor(out=r_cu[g][:, h], in0=r[g][:, h], in1=r_sq[g][:, h], op=ALU.mult)
+            nc.vector.tensor_tensor(out=r_cu[g][:, h], in0=r[g][:, h], in1=r_sq[g][:, h], op=ALU.mult)
 
         def grad(g):
             for h in halves:
@@ -146,7 +146,6 @@ def tile_rows_bagree_kernel(tc, x, w1, w2, so, wo, dy, old, out):
             nc.sync.dma_start(out=out[g, :, h], in_=res[g][:, h])
 
         whole = slice(0, N)
-        h0, h1 = halves
         copy_z2(0)
         make_prod(0)
         copy_z2(1)
@@ -154,42 +153,21 @@ def tile_rows_bagree_kernel(tc, x, w1, w2, so, wo, dy, old, out):
         roots(0)
         interleave(nc.vector.tensor_copy, dyq, 0, N)
         copy_z2(2)
+        copy_z2(3)
         make_prod(2)
         quantize(dyq)
-        product(bank_b[0], 0, woq, dyq)
-        product(bank_b[1], 1, woq, dyq)
-        product(bank_b[2], 2, woq, dyq)
-        cube(0, h0)
-        cube(0, h1)
-        roots(1)
-        grad(0)
-        copy_z2(3)
         make_prod(3)
-        product(bank_b[3], 3, woq, dyq)
-        add_old(nc.gpsimd, 0, h0)
-        cube(1, h0)
-        cube(1, h1)
-        add_old(nc.gpsimd, 0, h1)
-        store(0, whole)
-        roots(2)
-        grad(1)
-        add_old(nc.gpsimd, 1, h0)
-        cube(2, h0)
-        cube(2, h1)
-        add_old(nc.gpsimd, 1, h1)
-        store(1, whole)
-        nc.vector.scalar_tensor_tensor(
-            out=r_cu[3][:], in0=bank_b[3][:], scalar=soft(3), in1=z2[3][:], op0=ALU.mult, op1=ALU.mult
-        )
-        roots(3)
-        grad(2)
-        add_old(nc.gpsimd, 2, h0)
-        add_old(nc.gpsimd, 2, h1)
-        store(2, whole)
-        for h in halves:
-            nc.vector.tensor_tensor(out=t[3][:, h], in0=r_cu[3][:, h], in1=r[3][:, h], op=ALU.mult)
-        for h in halves:
-            nc.vector.tensor_tensor(out=dz1[3][:, h], in0=t[3][:, h], in1=r_sq[3][:, h], op=ALU.mult)
-        for h in halves:
-            add_old(nc.vector, 3, h)
-            store(3, h)
+        for g in range(G):
+            product(bank_b[g], g, woq, dyq)
+        for g in range(G):
+            if g + 1 < G:
+                roots(g + 1)
+            for h in halves:
+                cube(g, h)
+            grad(g)
+            for h in halves:
+                add_old(nc.vector, g, h)
+                if g == G - 1:
+                    store(g, h)
+            if g < G - 1:
+                store(g, whole)

@@ -17,7 +17,8 @@ P = 128
 PACK = 4
 ROWS = D // PACK
 HALF = N // 2
-X_SPLIT = 352
+X_SPLIT = 400
+DY_SPLIT = 256
 
 
 def tile_rows_bagree_kernel(tc, x, w1, w2, so, wo, dy, old, out):
@@ -91,11 +92,12 @@ def tile_rows_bagree_kernel(tc, x, w1, w2, so, wo, dy, old, out):
         prod_sq = tiles("prod_sq")
         r = tiles("r")
         r_sq = tiles("r_sq")
-        r_cu = tiles("r_cu")
+        u = tiles("u")
         t = tiles("t")
         dz1 = tiles("dz1")
         res = tiles("res")
         halves = [slice(0, HALF), slice(HALF, N)]
+        whole = slice(0, N)
 
         def soft(g):
             return so_cols[:, 32 * g : 32 * g + 1]
@@ -103,11 +105,11 @@ def tile_rows_bagree_kernel(tc, x, w1, w2, so, wo, dy, old, out):
         interleave(nc.vector.tensor_copy, xq, 0, X_SPLIT)
         interleave(nc.scalar.copy, xq, X_SPLIT, N)
         interleave(nc.scalar.copy, w2q, 0, M)
+        interleave(nc.scalar.copy, w1q, 0, M)
         quantize(xq)
-        interleave(nc.vector.tensor_copy, w1q, 0, M)
         quantize(w2q)
         quantize(w1q)
-        interleave(nc.scalar.copy, woq, 0, M)
+        interleave(nc.vector.tensor_copy, woq, 0, M)
         nc.vector.transpose(out=so_cols[:], in_=so_rows[:])
         quantize(woq)
         for g in range(G):
@@ -120,54 +122,67 @@ def tile_rows_bagree_kernel(tc, x, w1, w2, so, wo, dy, old, out):
         def make_prod(g):
             nc.vector.tensor_tensor(out=prod[g][:], in0=bank_b[g][:], in1=z2[g][:], op=ALU.mult)
 
-        def roots(g):
-            for h in halves:
-                nc.scalar.activation(out=prod_sq[g][:, h], in_=prod[g][:, h], func=ACT.Square)
-            for h in halves:
-                nc.scalar.activation(out=r[g][:, h], in_=prod_sq[g][:, h], func=ACT.Abs_reciprocal_sqrt, bias=soft(g))
-            for h in halves:
-                nc.scalar.activation(out=r_sq[g][:, h], in_=r[g][:, h], func=ACT.Square)
+        def square(g):
+            nc.scalar.activation(out=prod_sq[g][:], in_=prod[g][:], func=ACT.Square)
 
-        def cube(g, h):
-            nc.vector.tensor_tensor(out=r_cu[g][:, h], in0=r[g][:, h], in1=r_sq[g][:, h], op=ALU.mult)
+        def root(g):
+            nc.scalar.activation(out=r[g][:], in_=prod_sq[g][:], func=ACT.Abs_reciprocal_sqrt, bias=soft(g))
 
-        def grad(g):
-            for h in halves:
-                nc.vector.scalar_tensor_tensor(
-                    out=t[g][:, h], in0=bank_a[g][:, h], scalar=soft(g), in1=r_cu[g][:, h], op0=ALU.mult, op1=ALU.mult
-                )
-            for h in halves:
-                nc.vector.tensor_tensor(out=dz1[g][:, h], in0=bank_b[g][:, h], in1=t[g][:, h], op=ALU.mult)
+        def root_sq(g):
+            nc.scalar.activation(out=r_sq[g][:], in_=r[g][:], func=ACT.Square)
 
-        def add_old(eng, g, h):
-            eng.tensor_tensor(out=res[g][:, h], in0=dz1[g][:, h], in1=old_sb[:, g, h], op=ALU.add)
+        def make_u(g):
+            nc.vector.scalar_tensor_tensor(
+                out=u[g][:], in0=bank_b[g][:], scalar=soft(g), in1=z2[g][:], op0=ALU.mult, op1=ALU.mult
+            )
 
-        def store(g, h):
+        def make_t(g):
+            nc.vector.tensor_tensor(out=t[g][:], in0=u[g][:], in1=r[g][:], op=ALU.mult)
+
+        def make_dz1(g, h):
+            nc.vector.tensor_tensor(out=dz1[g][:, h], in0=t[g][:, h], in1=r_sq[g][:, h], op=ALU.mult)
+
+        def finish(g, h):
+            nc.vector.tensor_tensor(out=res[g][:, h], in0=dz1[g][:, h], in1=old_sb[:, g, h], op=ALU.add)
             nc.sync.dma_start(out=out[g, :, h], in_=res[g][:, h])
 
-        whole = slice(0, N)
         copy_z2(0)
         make_prod(0)
         copy_z2(1)
         make_prod(1)
-        roots(0)
-        interleave(nc.vector.tensor_copy, dyq, 0, N)
+        interleave(nc.scalar.copy, dyq, DY_SPLIT, N)
+        interleave(nc.vector.tensor_copy, dyq, 0, DY_SPLIT)
+        quantize(dyq)
         copy_z2(2)
         copy_z2(3)
         make_prod(2)
-        quantize(dyq)
         make_prod(3)
         for g in range(G):
             product(bank_b[g], g, woq, dyq)
-        for g in range(G):
-            if g + 1 < G:
-                roots(g + 1)
-            for h in halves:
-                cube(g, h)
-            grad(g)
-            for h in halves:
-                add_old(nc.vector, g, h)
-                if g == G - 1:
-                    store(g, h)
+        square(0)
+        square(1)
+        root(0)
+        root(1)
+        root_sq(0)
+        square(2)
+        root_sq(1)
+        root(2)
+        square(3)
+        root_sq(2)
+        root(3)
+        root_sq(3)
+        make_u(0)
+        make_u(1)
+        make_t(0)
+        make_u(2)
+        make_dz1(0, whole)
+        make_u(3)
+        for g in range(1, G):
+            make_t(g)
+            finish(g - 1, whole)
             if g < G - 1:
-                store(g, whole)
+                make_dz1(g, whole)
+        for h in halves:
+            make_dz1(G - 1, h)
+        for h in halves:
+            finish(G - 1, h)

from contextlib import ExitStack

import concourse.mybir as mybir

G, D, M, N = 4, 128, 128, 512
FLOPS = 3 * 2 * G * D * M * N

F32 = mybir.dt.float32
BF16 = mybir.dt.bfloat16
U32 = mybir.dt.uint32
U8 = mybir.dt.uint8
FP8X4 = mybir.dt.float8_e4m3fn_x4
ALU = mybir.AluOpType
ACT = mybir.ActivationFunctionType

P = 128
PACK = 4
ROWS = D // PACK
HALF = N // 2
X_SPLIT = 400
DY_SPLIT = 256


def tile_rows_bagree_kernel(tc, x, w1, w2, so, wo, dy, old, out):
    nc = tc.nc
    with ExitStack() as ctx:
        sb = ctx.enter_context(tc.tile_pool(name="sb", bufs=1))
        ps = ctx.enter_context(tc.psum_pool(name="ps", bufs=1))
        ctx.enter_context(tc.manual_schedule())

        def load(name, src):
            width = src.shape[2]
            raw = sb.tile([P, PACK, width], F32, name=name + "_raw", align_bytes=64)
            nc.sync.dma_start(out=raw[:], in_=src.rearrange("g (p j) w -> (g p) j w", j=PACK))
            grouped = sb.tile([P, width, PACK], BF16, name=name + "_bf", align_bytes=64)
            codes = sb.tile([P, width], U32, name=name + "_codes", align_bytes=64)
            scales = sb.tile([P, width], U8, name=name + "_scales", align_bytes=64)
            return raw, grouped, codes, scales

        def interleave(copy, op, lo, hi):
            raw, grouped = op[0], op[1]
            copy(
                out=grouped[:, lo:hi, :].rearrange("p (c i) j -> p c j i", i=4),
                in_=raw[:, :, lo:hi].rearrange("p j (c i) -> p c j i", i=4),
            )

        def quantize(op):
            nc.vector.quantize_mx(
                out=op[2][:].bitcast(FP8X4), scales=op[3][:], in_=op[1][:].rearrange("p w j -> p (w j)")
            )

        def product(bank, g, w, a):
            rows = slice(ROWS * g, ROWS * (g + 1))
            nc.tensor.matmul_mx(
                out=bank[:],
                lhsT=w[2][rows, :].bitcast(FP8X4),
                lhsT_scale=w[3][rows, :],
                rhs=a[2][rows, :].bitcast(FP8X4),
                rhs_scale=a[3][rows, :],
                start=True,
                stop=True,
            )

        so_rows = sb.tile([P, P], F32, align_bytes=64)
        so_cols = sb.tile([P, P], F32, align_bytes=64)
        nc.vector.memset(so_rows[:], 0.0)
        nc.scalar.dma_start(
            out=so_rows[0:P:32, :].rearrange("q (g i) -> q g i", g=G),
            in_=so.rearrange("g (q i) o -> q g (i o)", i=32),
        )
        warm_in = sb.tile([P, 8], F32)
        warm_out = sb.tile([P, 8], F32)
        nc.vector.memset(warm_in[:], 1.0)
        nc.scalar.activation(out=warm_out[:], in_=warm_in[:], func=ACT.Abs_reciprocal_sqrt)

        xq = load("x", x)
        w2q = load("w2", w2)
        w1q = load("w1", w1)
        woq = load("wo", wo)
        dyq = load("dy", dy)
        old_sb = sb.tile([P, G, N], F32)
        nc.sync.dma_start(out=old_sb[:], in_=old.rearrange("g m n -> m g n"))

        bank_a = [ps.tile([P, N], F32, name="bank_a%d" % g) for g in range(G)]
        bank_b = [ps.tile([P, N], F32, name="bank_b%d" % g) for g in range(G)]

        def tiles(name):
            return [sb.tile([P, N], F32, name="%s%d" % (name, g)) for g in range(G)]

        z2 = tiles("z2")
        prod = tiles("prod")
        prod_sq = tiles("prod_sq")
        r = tiles("r")
        r_sq = tiles("r_sq")
        u = tiles("u")
        t = tiles("t")
        dz1 = tiles("dz1")
        res = tiles("res")
        halves = [slice(0, HALF), slice(HALF, N)]
        whole = slice(0, N)

        def soft(g):
            return so_cols[:, 32 * g : 32 * g + 1]

        interleave(nc.vector.tensor_copy, xq, 0, X_SPLIT)
        interleave(nc.scalar.copy, xq, X_SPLIT, N)
        interleave(nc.scalar.copy, w2q, 0, M)
        interleave(nc.scalar.copy, w1q, 0, M)
        quantize(xq)
        quantize(w2q)
        quantize(w1q)
        interleave(nc.vector.tensor_copy, woq, 0, M)
        nc.vector.transpose(out=so_cols[:], in_=so_rows[:])
        quantize(woq)
        for g in range(G):
            product(bank_a[g], g, w2q, xq)
            product(bank_b[g], g, w1q, xq)

        def copy_z2(g):
            nc.scalar.copy(out=z2[g][:], in_=bank_a[g][:])

        def make_prod(g):
            nc.vector.tensor_tensor(out=prod[g][:], in0=bank_b[g][:], in1=z2[g][:], op=ALU.mult)

        def square(g):
            nc.scalar.activation(out=prod_sq[g][:], in_=prod[g][:], func=ACT.Square)

        def root(g):
            nc.scalar.activation(out=r[g][:], in_=prod_sq[g][:], func=ACT.Abs_reciprocal_sqrt, bias=soft(g))

        def root_sq(g):
            nc.scalar.activation(out=r_sq[g][:], in_=r[g][:], func=ACT.Square)

        def make_u(g):
            nc.vector.scalar_tensor_tensor(
                out=u[g][:], in0=bank_b[g][:], scalar=soft(g), in1=z2[g][:], op0=ALU.mult, op1=ALU.mult
            )

        def make_t(g):
            nc.vector.tensor_tensor(out=t[g][:], in0=u[g][:], in1=r[g][:], op=ALU.mult)

        def make_dz1(g, h):
            nc.vector.tensor_tensor(out=dz1[g][:, h], in0=t[g][:, h], in1=r_sq[g][:, h], op=ALU.mult)

        def finish(g, h):
            nc.vector.tensor_tensor(out=res[g][:, h], in0=dz1[g][:, h], in1=old_sb[:, g, h], op=ALU.add)
            nc.sync.dma_start(out=out[g, :, h], in_=res[g][:, h])

        copy_z2(0)
        make_prod(0)
        copy_z2(1)
        make_prod(1)
        interleave(nc.scalar.copy, dyq, DY_SPLIT, N)
        interleave(nc.vector.tensor_copy, dyq, 0, DY_SPLIT)
        quantize(dyq)
        copy_z2(2)
        copy_z2(3)
        make_prod(2)
        make_prod(3)
        for g in range(G):
            product(bank_b[g], g, woq, dyq)
        square(0)
        square(1)
        root(0)
        root(1)
        root_sq(0)
        square(2)
        root_sq(1)
        root(2)
        square(3)
        root_sq(2)
        root(3)
        root_sq(3)
        make_u(0)
        make_u(1)
        make_t(0)
        make_u(2)
        make_dz1(0, whole)
        make_u(3)
        for g in range(1, G):
            make_t(g)
            finish(g - 1, whole)
            if g < G - 1:
                make_dz1(g, whole)
        for h in halves:
            make_dz1(G - 1, h)
        for h in halves:
            finish(G - 1, h)
